import numpy as np
import ml_dtypes


def mxq(x, axis, fmt="e4m3"):
    dtype, down = {"e4m3": (ml_dtypes.float8_e4m3fn, 7), "e5m2": (ml_dtypes.float8_e5m2, 14)}[fmt]
    v = np.moveaxis(np.asarray(x, np.float32).astype(ml_dtypes.bfloat16).astype(np.float64), axis, -1)
    blocks = v.reshape(v.shape[:-1] + (-1, 32))
    amax = np.abs(blocks).max(-1, keepdims=True)
    byte = np.maximum(np.where(amax > 0, np.frexp(amax)[1] - 1 + 127, 0) - down, 1)
    scale = np.exp2(byte - 127.0)
    codes = (blocks / scale).astype(np.float32).astype(dtype).astype(np.float64)
    return np.moveaxis((codes * scale).reshape(v.shape), -1, axis)


WIDE = False


def mx_kscale(k):
    if not WIDE:
        return np.ones(k)
    levels = np.array([10, -10, 5, -5, 0])
    if k % 512:
        return np.exp2(np.random.permutation(np.resize(levels, k // 32))).repeat(32)
    a = np.empty((k // 512, 16))
    for p in range(k // 512):
        a[p, :8] = np.random.permutation(np.resize(levels, 8))
        for g in range(8):
            far = levels[np.abs(levels - a[p, g]) >= 10]
            a[p, g + 8] = far[np.random.randint(len(far))]
    return np.exp2(a.ravel()).repeat(32)


def f64(x):
    return np.asarray(x).astype(np.float64)


def striped(idx):
    return np.tile(np.asarray(idx).reshape(-1, 16).T, (8, 1)).astype(np.uint16)


def unstriped(offs):
    return offs[:16].T.reshape(-1).astype(np.int64)


def striped8(idx):
    return np.asarray(idx).reshape(8, -1, 16).transpose(0, 2, 1).reshape(128, -1).astype(np.uint16)


def unstriped8(offs):
    return offs.reshape(8, 16, -1).transpose(0, 2, 1).reshape(8, -1).astype(np.int64)


def pick8(x, idx, run):
    r = np.arange(len(x))
    return x[r[:, None], idx[r % (8 * run) // run]]


E2M1 = np.array([0.0, 0.5, 1.0, 1.5, 2.0, 3.0, 4.0, 6.0, -0.0, -0.5, -1.0, -1.5, -2.0, -3.0, -4.0, -6.0])


def pack_weight(w, fmt):
    k, n = w.shape
    w = f64(np.asarray(w, np.float32).astype(ml_dtypes.bfloat16)).reshape(k // 32, 32, n)
    amax = np.abs(w).max(1)
    if fmt == "e4m3":
        byte = np.frexp(amax)[1] - 1 + 127 - 7
    else:
        mant, ex = np.frexp(amax / 6.0)
        byte = np.where(mant > 0.5, ex, ex - 1) + 127
    byte = np.clip(np.where(amax > 0, byte, 1), 1, 254)
    scaled = (w * np.exp2(127.0 - byte)[:, None, :]).reshape(k, n).astype(np.float32)
    by_word = np.ascontiguousarray(scaled.reshape(k // 512, 128, 4, n).transpose(0, 1, 3, 2))
    if fmt == "e4m3":
        words = by_word.astype(ml_dtypes.float8_e4m3fn).view(np.uint8)
    else:
        c = by_word.astype(ml_dtypes.float4_e2m1fn).view(np.uint8) & 0xF
        words = (c[..., 0::2] | (c[..., 1::2] << 4)).reshape(k // 512, 128, 2 * n)
    return np.ascontiguousarray(words), np.ascontiguousarray(byte.astype(np.uint8).reshape(k // 512, 16, n))


def unpack_weight(words, scales, fmt):
    g, _, n = scales.shape
    words = np.ascontiguousarray(words).reshape(g, 128, n, -1)
    if fmt == "e4m3":
        vals = words.view(ml_dtypes.float8_e4m3fn).astype(np.float64)
    else:
        nib = np.empty((g, 128, n, 4), np.uint8)
        nib[..., 0::2] = words & 0xF
        nib[..., 1::2] = words >> 4
        vals = E2M1[nib]
    vals = vals * np.repeat(np.exp2(scales.astype(np.float64) - 127.0), 8, axis=1)[..., None]
    return vals.transpose(0, 1, 3, 2).reshape(g * 512, n)


def sgn(shape):
    return np.random.uniform(0.5, 2.0, shape) * np.where(np.random.standard_normal(shape) < 0, -1.0, 1.0)


K, J, R, T, F, S, O, N, Z, W = 512, 512, 512, 2048, 1024, 256, 128, 256, 1024, 512


def setup_inputs():
    n = np.random.standard_normal
    idx = np.stack([np.random.permutation(T)[:J] for _ in range(8)])
    idx2 = np.stack([np.random.permutation(T)[:J] for _ in range(8)])
    idx3 = np.random.permutation(F)[:R]
    idx4 = np.stack([np.random.permutation(J)[:S] for _ in range(8)])
    idx5 = np.random.permutation(J)[:S]
    idx6 = np.stack([np.random.permutation(Z)[:W] for _ in range(8)])
    idx7 = np.random.permutation(W)[:N]
    fk = mx_kscale(K)
    fr = mx_kscale(R)
    tr = np.ones(F)
    tr[idx3] = fr
    wtp = pack_weight(n((K, F)) * 1 / np.sqrt(K) / fk[:, None] * tr, "e2m1")
    return {
        "ta": (np.random.randint(-7, 8, (K, T)).astype(np.float64)).astype(np.float32),
        "ga": ((np.random.randint(10, 25, (K, 1)) / 64.0) * fk[:, None]).astype(np.float32),
        "gb": ((np.random.randint(4, 13, (K, 1)) / 64.0) * fk[:, None]).astype(np.float32),
        "wt_words": wtp[0],
        "wt_scales": wtp[1],
        "sa": (sgn((R, 1))).astype(np.float32),
        "sb": (sgn((R, 1))).astype(np.float32),
        "va": (np.random.randint(-7, 8, (R, Z)).astype(np.float64)).astype(np.float32),
        "ea": ((np.random.randint(8, 25, (R, 1)) / 1024.0) / fr[:, None]).astype(np.float32),
        "eb": (np.random.uniform(0.5, 1.6, (R, 1))).astype(np.float32),
        "offs": striped8(idx),
        "offs2": striped8(idx2),
        "offs3": striped(idx3),
        "offs4": striped8(idx4),
        "offs5": striped(idx5),
        "offs6": striped8(idx6),
        "offs7": striped(idx7),
    }


def reference(ta, ga, gb, wt_words, wt_scales, sa, sb, va, ea, eb, offs, offs2, offs3, offs4, offs5, offs6, offs7):
    idx = unstriped8(offs)
    idx2 = unstriped8(offs2)
    idx3 = unstriped(offs3)
    idx4 = unstriped8(offs4)
    idx5 = unstriped(offs5)
    idx6 = unstriped8(offs6)
    idx7 = unstriped(offs7)
    wtu = unpack_weight(wt_words, wt_scales, "e2m1")
    xc = pick8(f64(ta), idx, 64) * f64(ga) + pick8(f64(ta), idx2, 64) * f64(gb)
    wtidx3g = wtu[:, idx3]
    xcq = mxq(xc, 0, "e4m3")
    a = wtidx3g.T @ xcq
    h1 = np.maximum(pick8(a, idx4, 64) * f64(sa), a[:, idx5] * f64(sb))
    hid = h1.reshape(R, O, S // O).max(axis=2)
    vcd = pick8(f64(va), idx6, 64) * f64(ea)
    vc = vcd[:, idx7] * f64(eb)
    vcq = mxq(vc, 0, "e4m3")
    hidq = mxq(hid, 0, "e4m3")
    y = vcq.T @ hidq
    return y

@@ -1,0 +1,200 @@
+from contextlib import ExitStack
+
+import concourse.mybir as mybir
+
+K, J, R, T, F, S, O, N, Z, W = 512, 512, 512, 2048, 1024, 256, 128, 256, 1024, 512
+FLOPS = 2 * K * R * J + 2 * R * N * O
+
+F32 = mybir.dt.float32
+BF16 = mybir.dt.bfloat16
+I32 = mybir.dt.int32
+U32 = mybir.dt.uint32
+U16 = mybir.dt.uint16
+U8 = mybir.dt.uint8
+FP8X4 = mybir.dt.float8_e4m3fn_x4
+FP4X4 = mybir.dt.float4_e2m1fn_x4
+COPY = mybir.ActivationFunctionType.Copy
+ADD = mybir.AluOpType.add
+MAX = mybir.AluOpType.max
+XY = mybir.AxisListType.XY
+
+P = 128
+PACK = 4
+HALF = J // 2
+EARLY = 2
+
+
+def tile_picked_refined_store_one_pooledgroups_respelled_plain_kernel(
+    tc, ta, ga, gb, wt_words, wt_scales, sa, sb, va, ea, eb,
+    offs, offs2, offs3, offs4, offs5, offs6, offs7, out,
+):
+    nc = tc.nc
+    with ExitStack() as ctx:
+        keep = ctx.enter_context(tc.tile_pool(name="keep", bufs=1))
+        psum = ctx.enter_context(tc.psum_pool(name="psum", bufs=1))
+
+        def load_list(src, name):
+            tile = keep.tile(list(src.shape), U16, name=name)
+            nc.sync.dma_start(tile[:], src)
+            return tile
+
+        def load_factors(src, name, queue=nc.sync, first=0, count=PACK):
+            tile = keep.tile([P, count], F32, name=name)
+            queue.dma_start(tile[:], src.rearrange("(p t) one -> p (t one)", t=PACK)[:, first : first + count])
+            return tile
+
+        def load_rows(src, t, name):
+            tile = keep.tile([P, src.shape[1]], F32, name=name + str(t))
+            nc.sync.dma_start(tile[:], src.rearrange("(p t) c -> t p c", t=PACK)[t])
+            return tile
+
+        def fetch(dst, window, offsets, factors, t):
+            nc.scalar.activation(out=dst, in_=window[:].indirect(offsets), func=COPY, scale=factors[:, t : t + 1])
+
+        list6 = load_list(offs6, "list6")
+        ea_sb = load_factors(ea, "ea_sb", queue=nc.scalar)
+        va_rows = [load_rows(va, t, "va_rows") for t in range(EARLY)]
+        list7 = load_list(offs7, "list7")
+        eb_early = load_factors(eb, "eb_early", count=EARLY)
+        list3 = load_list(offs3, "list3")
+        scale_stage = keep.tile([4, 4, F], U8, name="scale_stage")
+        nc.sync.dma_start(
+            scale_stage[:].bitcast(I32), wt_scales[0].rearrange("(q r) c -> r q c", r=4).bitcast(I32)
+        )
+        list1 = load_list(offs, "list1")
+        ga_sb = load_factors(ga, "ga_sb")
+        ta_rows = [load_rows(ta, 0, "ta_rows")]
+        list2 = load_list(offs2, "list2")
+        gb_sb = load_factors(gb, "gb_sb")
+        word_store = keep.tile([P, F], U16, name="word_store")
+        nc.sync.dma_start(word_store[:].bitcast(I32), wt_words[0].bitcast(I32))
+        for t in range(1, PACK):
+            ta_rows.append(load_rows(ta, t, "ta_rows"))
+        for t in range(EARLY, PACK):
+            va_rows.append(load_rows(va, t, "va_rows"))
+        eb_late = load_factors(eb, "eb_late", first=EARLY, count=PACK - EARLY)
+        list4 = load_list(offs4, "list4")
+        sa_sb = load_factors(sa, "sa_sb")
+        list5 = load_list(offs5, "list5")
+        sb_sb = load_factors(sb, "sb_sb")
+
+        vc_planes = keep.tile([P, PACK, N], BF16, name="vc_planes")
+
+        def spell(planes, eb_part):
+            vcd = [keep.tile([P, W], F32, name="vcd" + str(t)) for t in planes]
+            for u, t in enumerate(planes):
+                fetch(vcd[u][:], va_rows[t], list6[:], ea_sb, t)
+            for u, t in enumerate(planes):
+                fetch(vc_planes[:, t, :], vcd[u], list7[:], eb_part, u)
+
+        spell(range(EARLY), eb_early)
+
+        scale_store = keep.tile([P, F], U8, name="scale_store")
+        nc.vector.memset(scale_store[:].bitcast(I32), 0)
+        for q in range(4):
+            nc.vector.tensor_copy(
+                out=scale_store[32 * q : 32 * q + 4, :].bitcast(I32), in_=scale_stage[:, q, :].bitcast(I32)
+            )
+        wt_scale = keep.tile([P, R], U8, name="wt_scale", align_bytes=64)
+        nc.vector.tensor_copy(
+            out=wt_scale[:].rearrange("p (t m) -> p m t", t=PACK), in_=scale_store[:].indirect(list3[:])
+        )
+        word_picked = keep.tile([P, R], U16, name="word_picked")
+        nc.vector.tensor_copy(out=word_picked[:], in_=word_store[:].indirect(list3[:]))
+        wt_word = keep.tile([P, 2 * R], U8, name="wt_word", align_bytes=64)
+        nc.vector.tensor_copy(
+            out=wt_word[:].rearrange("p (t m b) -> p t m b", t=PACK, b=2),
+            in_=word_picked[:].bitcast(U8).rearrange("p (m t b) -> p t m b", t=PACK, b=2),
+        )
+
+        xc = [keep.tile([P, HALF, PACK], BF16, name="xc" + str(h), align_bytes=64) for h in range(2)]
+        for t in range(PACK):
+            coarse = keep.tile([P, J], F32, name="coarse" + str(t))
+            fine = keep.tile([P, J], F32, name="fine" + str(t))
+            fetch(coarse[:], ta_rows[t], list1[:], ga_sb, t)
+            fetch(fine[:], ta_rows[t], list2[:], gb_sb, t)
+            for h in range(2):
+                cols = slice(h * HALF, (h + 1) * HALF)
+                nc.vector.tensor_tensor(out=xc[h][:, :, t], in0=coarse[:, cols], in1=fine[:, cols], op=ADD)
+        xc_code = keep.tile([P, J], U32, name="xc_code", align_bytes=64)
+        xc_scale = keep.tile([P, J], U8, name="xc_scale", align_bytes=64)
+        for h in range(2):
+            cols = slice(h * HALF, (h + 1) * HALF)
+            nc.vector.quantize_mx(
+                out=xc_code[:, cols].bitcast(FP8X4),
+                scales=xc_scale[:, cols],
+                in_=xc[h][:].rearrange("p j t -> p (j t)"),
+            )
+
+        spell(range(EARLY, PACK), eb_late)
+
+        hidden = []
+        for t in range(PACK):
+            a_rows = keep.tile([P, J], F32, name="a_rows" + str(t))
+            pieces = 2 if t == 0 else 1
+            width = J // pieces
+            for h in range(pieces):
+                cols = slice(h * width, (h + 1) * width)
+                acc = psum.tile([P, width], F32, name="acc%d_%d" % (t, h))
+                nc.tensor.matmul_mx(
+                    out=acc[:],
+                    lhsT=wt_word[:, 2 * P * t : 2 * P * (t + 1)].bitcast(FP4X4),
+                    lhsT_scale=wt_scale[:, P * t : P * (t + 1)],
+                    rhs=xc_code[:, cols].bitcast(FP8X4),
+                    rhs_scale=xc_scale[:, cols],
+                    start=True,
+                    stop=True,
+                )
+                nc.vector.tensor_copy(out=a_rows[:, cols], in_=acc[:])
+            hidden.append(a_rows)
+
+        vc = keep.tile([P, N, PACK], BF16, name="vc", align_bytes=64)
+        nc.vector.tensor_copy(
+            out=vc[:].rearrange("p (i m) t -> p i m t", i=2),
+            in_=vc_planes[:].rearrange("p t (m i) -> p i m t", i=2),
+        )
+        vc_code = keep.tile([P, N], U32, name="vc_code", align_bytes=64)
+        vc_scale = keep.tile([P, N], U8, name="vc_scale", align_bytes=64)
+        nc.vector.quantize_mx(
+            out=vc_code[:].bitcast(FP8X4), scales=vc_scale[:], in_=vc[:].rearrange("p n t -> p (n t)")
+        )
+
+        hid = keep.tile([P, O, PACK], BF16, name="hid", align_bytes=64)
+        for t in range(PACK):
+            picks = keep.tile([P, 2, S], F32, name="picks" + str(t))
+            fetch(picks[:, 0, :], hidden[t], list4[:], sa_sb, t)
+            pieces = 2 if t == PACK - 1 else 1
+            width = S // pieces
+            for h in range(pieces):
+                fetch(picks[:, 1, h * width : (h + 1) * width], hidden[t],
+                      list5[:, h * width // 16 : (h + 1) * width // 16], sb_sb, t)
+            for h in range(pieces):
+                nc.vector.tensor_reduce(
+                    out=hid[:, h * width // 2 : (h + 1) * width // 2, t],
+                    in_=picks[:, :, h * width : (h + 1) * width].rearrange("p u (o s) -> p o u s", s=2),
+                    axis=XY,
+                    op=MAX,
+                )
+        hid_code = keep.tile([P, O], U32, name="hid_code", align_bytes=64)
+        hid_scale = keep.tile([P, O], U8, name="hid_scale", align_bytes=64)
+        nc.vector.quantize_mx(
+            out=hid_code[:].bitcast(FP8X4), scales=hid_scale[:], in_=hid[:].rearrange("p o t -> p (o t)")
+        )
+
+        result = keep.tile([P, 2, O], F32, name="result")
+        for i in range(2):
+            acc = psum.tile([P, O], F32, name="acc_out" + str(i))
+            nc.tensor.matmul_mx(
+                out=acc[:],
+                lhsT=vc_code[:, P * i : P * (i + 1)].bitcast(FP8X4),
+                lhsT_scale=vc_scale[:, P * i : P * (i + 1)],
+                rhs=hid_code[:].bitcast(FP8X4),
+                rhs_scale=hid_scale[:],
+                start=True,
+                stop=True,
+            )
+            if i == 0:
+                nc.vector.tensor_copy(out=result[:, i, :], in_=acc[:])
+            else:
+                nc.scalar.copy(out=result[:, i, :], in_=acc[:])
+        nc.sync.dma_start(out.rearrange("(m i) o -> m i o", i=2), result[:])

@@ -78,6 +78,11 @@ def tile_picked_refined_store_one_pooledgroups_respelled_plain_kernel(
         list5 = load_list(offs5, "list5")
         sb_sb = load_factors(sb, "sb_sb")
 
+        warm_in = keep.tile([P, 1], F32, name="warm_in")
+        warm_out = keep.tile([P, 1], F32, name="warm_out")
+        nc.vector.memset(warm_in[:], 0.0)
+        nc.scalar.activation(out=warm_out[:], in_=warm_in[:], func=COPY)
+
         vc_planes = keep.tile([P, PACK, N], BF16, name="vc_planes")
 
         def spell(planes, eb_part):

@@ -56,20 +56,21 @@ def tile_picked_refined_store_one_pooledgroups_respelled_plain_kernel(
         va_rows = [load_rows(va, t, "va_rows") for t in range(EARLY)]
         list7 = load_list(offs7, "list7")
         eb_early = load_factors(eb, "eb_early", count=EARLY)
-        list3 = load_list(offs3, "list3")
-        scale_stage = keep.tile([4, 4, F], U8, name="scale_stage")
-        nc.sync.dma_start(
-            scale_stage[:].bitcast(I32), wt_scales[0].rearrange("(q r) c -> r q c", r=4).bitcast(I32)
-        )
         list1 = load_list(offs, "list1")
         ga_sb = load_factors(ga, "ga_sb")
         ta_rows = [load_rows(ta, 0, "ta_rows")]
         list2 = load_list(offs2, "list2")
         gb_sb = load_factors(gb, "gb_sb")
+        list3 = load_list(offs3, "list3")
+        scale_stage = keep.tile([4, 4, F], U8, name="scale_stage")
+        nc.sync.dma_start(
+            scale_stage[:].bitcast(I32), wt_scales[0].rearrange("(q r) c -> r q c", r=4).bitcast(I32)
+        )
+        for t in range(1, PACK - 1):
+            ta_rows.append(load_rows(ta, t, "ta_rows"))
         word_store = keep.tile([P, F], U16, name="word_store")
         nc.sync.dma_start(word_store[:].bitcast(I32), wt_words[0].bitcast(I32))
-        for t in range(1, PACK):
-            ta_rows.append(load_rows(ta, t, "ta_rows"))
+        ta_rows.append(load_rows(ta, PACK - 1, "ta_rows"))
         for t in range(EARLY, PACK):
             va_rows.append(load_rows(va, t, "va_rows"))
         eb_late = load_factors(eb, "eb_late", first=EARLY, count=PACK - EARLY)
@@ -104,6 +105,7 @@ def tile_picked_refined_store_one_pooledgroups_respelled_plain_kernel(
         nc.vector.tensor_copy(
             out=wt_scale[:].rearrange("p (t m) -> p m t", t=PACK), in_=scale_store[:].indirect(list3[:])
         )
+
         word_picked = keep.tile([P, R], U16, name="word_picked")
         nc.vector.tensor_copy(out=word_picked[:], in_=word_store[:].indirect(list3[:]))
         wt_word = keep.tile([P, 2 * R], U8, name="wt_word", align_bytes=64)
@@ -112,7 +114,7 @@ def tile_picked_refined_store_one_pooledgroups_respelled_plain_kernel(
             in_=word_picked[:].bitcast(U8).rearrange("p (m t b) -> p t m b", t=PACK, b=2),
         )
 
-        xc = [keep.tile([P, HALF, PACK], BF16, name="xc" + str(h), align_bytes=64) for h in range(2)]
+        pairs = [keep.tile([P, 2, HALF, 2], BF16, name="pairs" + str(h)) for h in range(2)]
         for t in range(PACK):
             coarse = keep.tile([P, J], F32, name="coarse" + str(t))
             fine = keep.tile([P, J], F32, name="fine" + str(t))
@@ -120,7 +122,13 @@ def tile_picked_refined_store_one_pooledgroups_respelled_plain_kernel(
             fetch(fine[:], ta_rows[t], list2[:], gb_sb, t)
             for h in range(2):
                 cols = slice(h * HALF, (h + 1) * HALF)
-                nc.vector.tensor_tensor(out=xc[h][:, :, t], in0=coarse[:, cols], in1=fine[:, cols], op=ADD)
+                nc.vector.tensor_tensor(out=pairs[h][:, t // 2, :, t % 2], in0=coarse[:, cols], in1=fine[:, cols], op=ADD)
+        xc = [keep.tile([P, HALF * PACK], BF16, name="xc" + str(h), align_bytes=64) for h in range(2)]
+        for h in range(2):
+            nc.vector.tensor_copy(
+                out=xc[h][:].bitcast(I32).rearrange("p (j u) -> p j u", u=2),
+                in_=pairs[h][:].rearrange("p u j e -> p (u j e)").bitcast(I32).rearrange("p (u j) -> p j u", u=2),
+            )
         xc_code = keep.tile([P, J], U32, name="xc_code", align_bytes=64)
         xc_scale = keep.tile([P, J], U8, name="xc_scale", align_bytes=64)
         for h in range(2):
@@ -128,7 +136,7 @@ def tile_picked_refined_store_one_pooledgroups_respelled_plain_kernel(
             nc.vector.quantize_mx(
                 out=xc_code[:, cols].bitcast(FP8X4),
                 scales=xc_scale[:, cols],
-                in_=xc[h][:].rearrange("p j t -> p (j t)"),
+                in_=xc[h][:],
             )
 
         spell(range(EARLY, PACK), eb_late)

from contextlib import ExitStack

import concourse.mybir as mybir

K, J, R, T, F, S, O, N, Z, W = 512, 512, 512, 2048, 1024, 256, 128, 256, 1024, 512
FLOPS = 2 * K * R * J + 2 * R * N * O

F32 = mybir.dt.float32
BF16 = mybir.dt.bfloat16
I32 = mybir.dt.int32
U32 = mybir.dt.uint32
U16 = mybir.dt.uint16
U8 = mybir.dt.uint8
FP8X4 = mybir.dt.float8_e4m3fn_x4
FP4X4 = mybir.dt.float4_e2m1fn_x4
COPY = mybir.ActivationFunctionType.Copy
ADD = mybir.AluOpType.add
MAX = mybir.AluOpType.max
XY = mybir.AxisListType.XY

P = 128
PACK = 4
HALF = J // 2
EARLY = 2


def tile_picked_refined_store_one_pooledgroups_respelled_plain_kernel(
    tc, ta, ga, gb, wt_words, wt_scales, sa, sb, va, ea, eb,
    offs, offs2, offs3, offs4, offs5, offs6, offs7, out,
):
    nc = tc.nc
    with ExitStack() as ctx:
        keep = ctx.enter_context(tc.tile_pool(name="keep", bufs=1))
        psum = ctx.enter_context(tc.psum_pool(name="psum", bufs=1))

        def load_list(src, name):
            tile = keep.tile(list(src.shape), U16, name=name)
            nc.sync.dma_start(tile[:], src)
            return tile

        def load_factors(src, name, queue=nc.sync, first=0, count=PACK):
            tile = keep.tile([P, count], F32, name=name)
            queue.dma_start(tile[:], src.rearrange("(p t) one -> p (t one)", t=PACK)[:, first : first + count])
            return tile

        def load_rows(src, t, name):
            tile = keep.tile([P, src.shape[1]], F32, name=name + str(t))
            nc.sync.dma_start(tile[:], src.rearrange("(p t) c -> t p c", t=PACK)[t])
            return tile

        def fetch(dst, window, offsets, factors, t):
            nc.scalar.activation(out=dst, in_=window[:].indirect(offsets), func=COPY, scale=factors[:, t : t + 1])

        list6 = load_list(offs6, "list6")
        ea_sb = load_factors(ea, "ea_sb", queue=nc.scalar)
        va_rows = [load_rows(va, t, "va_rows") for t in range(EARLY)]
        list7 = load_list(offs7, "list7")
        eb_early = load_factors(eb, "eb_early", count=EARLY)
        list1 = load_list(offs, "list1")
        ga_sb = load_factors(ga, "ga_sb")
        ta_rows = [load_rows(ta, 0, "ta_rows")]
        list2 = load_list(offs2, "list2")
        gb_sb = load_factors(gb, "gb_sb")
        list3 = load_list(offs3, "list3")
        scale_stage = keep.tile([4, 4, F], U8, name="scale_stage")
        nc.sync.dma_start(
            scale_stage[:].bitcast(I32), wt_scales[0].rearrange("(q r) c -> r q c", r=4).bitcast(I32)
        )
        for t in range(1, PACK - 1):
            ta_rows.append(load_rows(ta, t, "ta_rows"))
        word_store = keep.tile([P, F], U16, name="word_store")
        nc.sync.dma_start(word_store[:].bitcast(I32), wt_words[0].bitcast(I32))
        ta_rows.append(load_rows(ta, PACK - 1, "ta_rows"))
        for t in range(EARLY, PACK):
            va_rows.append(load_rows(va, t, "va_rows"))
        eb_late = load_factors(eb, "eb_late", first=EARLY, count=PACK - EARLY)
        list4 = load_list(offs4, "list4")
        sa_sb = load_factors(sa, "sa_sb")
        list5 = load_list(offs5, "list5")
        sb_sb = load_factors(sb, "sb_sb")

        warm_in = keep.tile([P, 1], F32, name="warm_in")
        warm_out = keep.tile([P, 1], F32, name="warm_out")
        nc.vector.memset(warm_in[:], 0.0)
        nc.scalar.activation(out=warm_out[:], in_=warm_in[:], func=COPY)

        vc_planes = keep.tile([P, PACK, N], BF16, name="vc_planes")

        def spell(planes, eb_part):
            vcd = [keep.tile([P, W], F32, name="vcd" + str(t)) for t in planes]
            for u, t in enumerate(planes):
                fetch(vcd[u][:], va_rows[t], list6[:], ea_sb, t)
            for u, t in enumerate(planes):
                fetch(vc_planes[:, t, :], vcd[u], list7[:], eb_part, u)

        spell(range(EARLY), eb_early)

        scale_store = keep.tile([P, F], U8, name="scale_store")
        nc.vector.memset(scale_store[:].bitcast(I32), 0)
        for q in range(4):
            nc.vector.tensor_copy(
                out=scale_store[32 * q : 32 * q + 4, :].bitcast(I32), in_=scale_stage[:, q, :].bitcast(I32)
            )
        wt_scale = keep.tile([P, R], U8, name="wt_scale", align_bytes=64)
        nc.vector.tensor_copy(
            out=wt_scale[:].rearrange("p (t m) -> p m t", t=PACK), in_=scale_store[:].indirect(list3[:])
        )

        word_picked = keep.tile([P, R], U16, name="word_picked")
        nc.vector.tensor_copy(out=word_picked[:], in_=word_store[:].indirect(list3[:]))
        wt_word = keep.tile([P, 2 * R], U8, name="wt_word", align_bytes=64)
        nc.vector.tensor_copy(
            out=wt_word[:].rearrange("p (t m b) -> p t m b", t=PACK, b=2),
            in_=word_picked[:].bitcast(U8).rearrange("p (m t b) -> p t m b", t=PACK, b=2),
        )

        pairs = [keep.tile([P, 2, HALF, 2], BF16, name="pairs" + str(h)) for h in range(2)]
        for t in range(PACK):
            coarse = keep.tile([P, J], F32, name="coarse" + str(t))
            fine = keep.tile([P, J], F32, name="fine" + str(t))
            fetch(coarse[:], ta_rows[t], list1[:], ga_sb, t)
            fetch(fine[:], ta_rows[t], list2[:], gb_sb, t)
            for h in range(2):
                cols = slice(h * HALF, (h + 1) * HALF)
                nc.vector.tensor_tensor(out=pairs[h][:, t // 2, :, t % 2], in0=coarse[:, cols], in1=fine[:, cols], op=ADD)
        xc = [keep.tile([P, HALF * PACK], BF16, name="xc" + str(h), align_bytes=64) for h in range(2)]
        for h in range(2):
            nc.vector.tensor_copy(
                out=xc[h][:].bitcast(I32).rearrange("p (j u) -> p j u", u=2),
                in_=pairs[h][:].rearrange("p u j e -> p (u j e)").bitcast(I32).rearrange("p (u j) -> p j u", u=2),
            )
        xc_code = keep.tile([P, J], U32, name="xc_code", align_bytes=64)
        xc_scale = keep.tile([P, J], U8, name="xc_scale", align_bytes=64)
        for h in range(2):
            cols = slice(h * HALF, (h + 1) * HALF)
            nc.vector.quantize_mx(
                out=xc_code[:, cols].bitcast(FP8X4),
                scales=xc_scale[:, cols],
                in_=xc[h][:],
            )

        spell(range(EARLY, PACK), eb_late)

        hidden = []
        for t in range(PACK):
            a_rows = keep.tile([P, J], F32, name="a_rows" + str(t))
            pieces = 2 if t == 0 else 1
            width = J // pieces
            for h in range(pieces):
                cols = slice(h * width, (h + 1) * width)
                acc = psum.tile([P, width], F32, name="acc%d_%d" % (t, h))
                nc.tensor.matmul_mx(
                    out=acc[:],
                    lhsT=wt_word[:, 2 * P * t : 2 * P * (t + 1)].bitcast(FP4X4),
                    lhsT_scale=wt_scale[:, P * t : P * (t + 1)],
                    rhs=xc_code[:, cols].bitcast(FP8X4),
                    rhs_scale=xc_scale[:, cols],
                    start=True,
                    stop=True,
                )
                nc.vector.tensor_copy(out=a_rows[:, cols], in_=acc[:])
            hidden.append(a_rows)

        vc = keep.tile([P, N, PACK], BF16, name="vc", align_bytes=64)
        nc.vector.tensor_copy(
            out=vc[:].rearrange("p (i m) t -> p i m t", i=2),
            in_=vc_planes[:].rearrange("p t (m i) -> p i m t", i=2),
        )
        vc_code = keep.tile([P, N], U32, name="vc_code", align_bytes=64)
        vc_scale = keep.tile([P, N], U8, name="vc_scale", align_bytes=64)
        nc.vector.quantize_mx(
            out=vc_code[:].bitcast(FP8X4), scales=vc_scale[:], in_=vc[:].rearrange("p n t -> p (n t)")
        )

        hid = keep.tile([P, O, PACK], BF16, name="hid", align_bytes=64)
        for t in range(PACK):
            picks = keep.tile([P, 2, S], F32, name="picks" + str(t))
            fetch(picks[:, 0, :], hidden[t], list4[:], sa_sb, t)
            pieces = 2 if t == PACK - 1 else 1
            width = S // pieces
            for h in range(pieces):
                fetch(picks[:, 1, h * width : (h + 1) * width], hidden[t],
                      list5[:, h * width // 16 : (h + 1) * width // 16], sb_sb, t)
            for h in range(pieces):
                nc.vector.tensor_reduce(
                    out=hid[:, h * width // 2 : (h + 1) * width // 2, t],
                    in_=picks[:, :, h * width : (h + 1) * width].rearrange("p u (o s) -> p o u s", s=2),
                    axis=XY,
                    op=MAX,
                )
        hid_code = keep.tile([P, O], U32, name="hid_code", align_bytes=64)
        hid_scale = keep.tile([P, O], U8, name="hid_scale", align_bytes=64)
        nc.vector.quantize_mx(
            out=hid_code[:].bitcast(FP8X4), scales=hid_scale[:], in_=hid[:].rearrange("p o t -> p (o t)")
        )

        result = keep.tile([P, 2, O], F32, name="result")
        for i in range(2):
            acc = psum.tile([P, O], F32, name="acc_out" + str(i))
            nc.tensor.matmul_mx(
                out=acc[:],
                lhsT=vc_code[:, P * i : P * (i + 1)].bitcast(FP8X4),
                lhsT_scale=vc_scale[:, P * i : P * (i + 1)],
                rhs=hid_code[:].bitcast(FP8X4),
                rhs_scale=hid_scale[:],
                start=True,
                stop=True,
            )
            if i == 0:
                nc.vector.tensor_copy(out=result[:, i, :], in_=acc[:])
            else:
                nc.scalar.copy(out=result[:, i, :], in_=acc[:])
        nc.sync.dma_start(out.rearrange("(m i) o -> m i o", i=2), result[:])
